import numpy as np, ml_dtypes
CORES = [1,14,19,24,37,42,55,60,65,78,83,88,101,106,119,124]
N = 16
import mx_ref
NC, G, KO, SH = 256, 4, 2, 2
C = np.float32(0.043)
BF = ml_dtypes.bfloat16
def cut(t, i, w=512):
    return t[:, w * i:w * i + w]
def tile(rs):
    return np.stack(rs, axis=2).reshape(128, -1).astype(BF)
def layer(w, X):
    out = []
    for i in range(G):
        for t in range(len(X)):
            p = mx_ref.matmul(mx_ref.quantize(cut(w, len(X) * i + t)), X[t])
            z = p if t == 0 else z + p
        out.append(z)
    return out
def act(Z):
    return [np.maximum(z, 0) * C for z in Z]
def inputs(rng, e, E):
    def f(*shape):
        v = (rng.standard_normal(shape, dtype=np.float32) * np.exp2(rng.integers(-2, 3, shape[:-1] + (1,)))).astype(BF)
        return mx_ref.spread((v.astype(np.float32) * np.exp2(rng.integers(-E, E + 1, shape[:-2] + (1, 1))).astype(np.float32)).astype(BF), rng, e)
    def packed(k):
        c = np.zeros((N, 128, k * 512), np.uint8); s = np.zeros((N, 128, k * 128), np.uint8)
        for r in range(N):
            for i in range(k):
                a, b = mx_ref.quantize(f(128, 512)); c[r][:, 512 * i:512 * i + 512] = a; s[r][:, 128 * i:128 * i + 128] = mx_ref.plane(b, rng)
        return c, s
    d = {}
    d["kc"], d["ks"] = packed(KO)
    d["x"] = f(N, 128, 4 * NC)
    d["wk"] = f(N, 128, G * 512)
    d["q"] = f(N, 128, 512)
    return d
def setup_inputs(rng):
    return inputs(rng, 0, 0)
def setup_inputs_blocks(rng):
    return inputs(rng, 4, 0)
def setup_inputs_wide(rng):
    return inputs(rng, 0, 8)
def reference(kc, ks, x, wk, q):
    new = [mx_ref.quantize(tile(act(layer(wk[r], [mx_ref.quantize(x[r])])))) for r in range(N)]
    y = np.zeros((N, 128, 128 * KO + NC), np.float32)
    for o in range(N):
        old = (np.ascontiguousarray(kc[o]), mx_ref.live(ks[o]))
        qq = mx_ref.quantize(q[o])
        y[o] = np.concatenate([mx_ref.matmul(qq, old), mx_ref.matmul(qq, new[(o - SH) % N])], axis=1)
    return {"y": y}

import numpy as np
from concourse.mybir import dt, AluOpType, ActivationFunctionType

N, SH, C = 16, 2, float(np.float32(0.043))
H = 128
NC = 256

SCRATCH = {
    "xb": ("sbuf", [128, 4 * NC], "bfloat16"),
    "wb": ("sbuf", [128, 2048], "bfloat16"),
    "qb": ("sbuf", [128, 512], "bfloat16"),
    "xq": ("sbuf", [128, NC], "float8_e4m3fn_x4"),
    "xs": ("sbuf", [128, NC], "uint8"),
    "wq": ("sbuf", [128, 512], "float8_e4m3fn_x4"),
    "ws": ("sbuf", [128, 512], "uint8"),
    "qq": ("sbuf", [128, 128], "float8_e4m3fn_x4"),
    "qs": ("sbuf", [128, 128], "uint8"),
    "oc": ("sbuf", [128, NC], "float8_e4m3fn_x4"),
    "op": ("sbuf", [128, NC], "uint8"),
    "kt": ("sbuf", [128, 4 * NC], "bfloat16"),
    "kq": ("sbuf", [128, NC], "float8_e4m3fn_x4"),
    "kp": ("sbuf", [128, NC], "uint8"),
    "lc": ("sbuf", [128, NC], "float8_e4m3fn_x4"),
    "lp": ("sbuf", [128, NC], "uint8"),
    "yb": ("sbuf", [128, 2 * NC], "float32"),
    "ps": ("psum", [128, 512 * 8], "float32"),
}
SEMAPHORES = ["lx0", "lw0", "lw1", "lx1", "lq", "lk", "vq", "va", "sa", "tm", "sent_c", "sent_p", "arr", "stored"]


def rank_program(g, core, T, topo):
    rank = T.rank_of(core)
    if rank is None:
        return
    S = T.sem
    dst = T.cores[(rank + SH) % N]
    rid, pid = topo.addr(dst)[:2]
    mask = topo.mask(core, dst)
    ne = bin(mask).count("1")
    V, A, P, D = g.vector, g.scalar, g.tensor, g.sync

    def bank(i, n):
        return T.ps[:, 512 * i:512 * i + n]

    def kt(h, b):
        return T.kt[:, 4 * H * h + b:4 * H * (h + 1):4]

    D.dma_start(T.xb[:, 0:512], T.x[:, 0:512]).then_inc(S.lx0, 16)
    D.dma_start(T.wb[:, 0:1536], T.wk[:, 0:1536]).then_inc(S.lw0, 16)
    D.dma_start(T.wb[:, 1536:2048], T.wk[:, 1536:2048]).then_inc(S.lw1, 16)
    D.dma_start(T.xb[:, 512:1024], T.x[:, 512:1024]).then_inc(S.lx1, 16)
    D.dma_start(T.qb[:], T.q[:]).then_inc(S.lq, 16)
    D.dma_start(T.oc[:].bitcast(dt.uint8), T.kc[:]).then_inc(S.lk, 16)
    D.dma_start(T.op[:], T.ks[:]).then_inc(S.lk, 16)

    def quant_w(i):
        V.quantize_mx(T.wq[:, 128 * i:128 * i + 128], T.ws[:, 128 * i:128 * i + 128], T.wb[:, 512 * i:512 * i + 512]).then_inc(S.vq, 1)

    def quant_x(h):
        V.quantize_mx(T.xq[:, H * h:H * h + H], T.xs[:, H * h:H * h + H], T.xb[:, 512 * h:512 * h + 512]).then_inc(S.vq, 1)

    def quant_k(h):
        V.quantize_mx(T.kq[:, H * h:H * h + H], T.kp[:, H * h:H * h + H], T.kt[:, 512 * h:512 * h + 512]).then_inc(S.vq, 1)

    def rect_v(h, b):
        V.tensor_scalar(kt(h, b), bank(4 * h + b, H), 0.0, C, AluOpType.max, AluOpType.mult).then_inc(S.va, 1)

    def rect_a(h, b):
        A.activation(kt(h, b), bank(4 * h + b, H), ActivationFunctionType.Relu, scale=C).then_inc(S.sa, 1)

    V.wait_ge(S.lx0, 16)
    quant_x(0)
    V.wait_ge(S.lw0, 16)
    for i in range(3):
        quant_w(i)
    V.wait_ge(S.lw1, 16)
    quant_w(3)
    V.wait_ge(S.tm, 4)
    rect_v(0, 3)
    V.wait_ge(S.sa, 3)
    V.wait_ge(S.va, 1)
    quant_k(0)
    V.wait_ge(S.lx1, 16)
    quant_x(1)
    V.wait_ge(S.tm, 6)
    rect_v(1, 1)
    V.wait_ge(S.tm, 8)
    rect_v(1, 3)
    V.wait_ge(S.sa, 5)
    V.wait_ge(S.va, 3)
    quant_k(1)
    V.wait_ge(S.lq, 16)
    V.quantize_mx(T.qq[:], T.qs[:], T.qb[:]).then_inc(S.vq, 1)
    V.wait_ge(S.tm, 10)
    V.tensor_copy(T.yb[:, NC:NC + H], bank(1, H)).then_inc(S.va, 1)

    def product(h, b):
        P.matmul_mx(bank(4 * h + b, H), T.wq[:, 128 * b:128 * b + 128], T.ws[:, 128 * b:128 * b + 128],
                    T.xq[:, H * h:H * h + H], T.xs[:, H * h:H * h + H], True, True).then_inc(S.tm, 1)

    for b in range(4):
        P.wait_ge(S.vq, 2 + b)
        product(0, b)
    P.wait_ge(S.vq, 7)
    for b in range(4):
        product(1, b)
    P.wait_ge(S.lk, 32)
    P.wait_ge(S.vq, 9)
    P.wait_ge(S.sa, 3)
    P.matmul_mx(bank(0, NC), T.qq[:], T.qs[:], T.oc[:], T.op[:], True, True).then_inc(S.tm, 1)
    P.wait_ge(S.arr, 3 * ne)
    for h in range(2):
        P.matmul_mx(bank(1 + h, H), T.qq[:], T.qs[:], T.lc[:, H * h:H * h + H], T.lp[:, H * h:H * h + H], True, True).then_inc(S.tm, 1)

    for b in range(3):
        A.wait_ge(S.tm, 1 + b)
        rect_a(0, b)
    for b in (0, 2):
        A.wait_ge(S.tm, 5 + b)
        rect_a(1, b)
    A.wait_ge(S.tm, 9)
    A.activation(T.yb[:, 0:NC], bank(0, NC), ActivationFunctionType.Copy).then_inc(S.sa, 1)
    A.wait_ge(S.tm, 11)
    A.activation(T.yb[:, NC + H:2 * NC], bank(2, H), ActivationFunctionType.Copy).then_inc(S.sa, 1)

    def send_codes(h):
        g.remote_dma(T.lc[:, H * h:H * h + H].bitcast(dt.uint8), T.kq[:, H * h:H * h + H].bitcast(dt.uint8),
                     S.arr, S.sent_c, pid, rid, mask)

    g.wait_ge(S.vq, 6)
    send_codes(0)
    g.wait_ge(S.vq, 8)
    send_codes(1)
    g.remote_dma(T.lp[:], T.kp[:], S.arr, S.sent_p, pid, rid, mask)
    g.wait_ge(S.sent_p, ne)

    D.wait_ge(S.sa, 6)
    D.wait_ge(S.sent_c, 2 * ne)
    D.dma_start(T.y[:, 0:NC], T.yb[:, 0:NC]).then_inc(S.stored, 16)
    D.wait_ge(S.va, 4)
    D.wait_ge(S.sa, 7)
    D.dma_start(T.y[:, NC:2 * NC], T.yb[:, NC:2 * NC]).then_inc(S.stored, 16)
    D.wait_ge(S.stored, 32)
